import numpy as np
import ml_dtypes


def mxq(x, axis, fmt="e4m3"):
    dtype, down = {"e4m3": (ml_dtypes.float8_e4m3fn, 7), "e5m2": (ml_dtypes.float8_e5m2, 14)}[fmt]
    v = np.moveaxis(np.asarray(x, np.float32).astype(ml_dtypes.bfloat16).astype(np.float64), axis, -1)
    blocks = v.reshape(v.shape[:-1] + (-1, 32))
    amax = np.abs(blocks).max(-1, keepdims=True)
    byte = np.maximum(np.where(amax > 0, np.frexp(amax)[1] - 1 + 127, 0) - down, 1)
    scale = np.exp2(byte - 127.0)
    codes = (blocks / scale).astype(np.float32).astype(dtype).astype(np.float64)
    return np.moveaxis((codes * scale).reshape(v.shape), -1, axis)


WIDE = False


def mx_kscale(k):
    if not WIDE:
        return np.ones(k)
    levels = np.array([10, -10, 5, -5, 0])
    if k % 512:
        return np.exp2(np.random.permutation(np.resize(levels, k // 32))).repeat(32)
    a = np.empty((k // 512, 16))
    for p in range(k // 512):
        a[p, :8] = np.random.permutation(np.resize(levels, 8))
        for g in range(8):
            far = levels[np.abs(levels - a[p, g]) >= 10]
            a[p, g + 8] = far[np.random.randint(len(far))]
    return np.exp2(a.ravel()).repeat(32)


def f64(x):
    return np.asarray(x).astype(np.float64)


def striped(idx):
    return np.tile(idx.reshape(-1, 16).T, (8, 1)).astype(np.uint16)


def unstriped(offs):
    return offs[:16].T.reshape(-1).astype(np.int64)


def striped8(idx):
    return np.concatenate([x.reshape(-1, 16).T for x in idx]).astype(np.uint16)


def runs(offs, k):
    lists = np.stack([offs[16 * r : 16 * r + 16].T.reshape(-1) for r in range(8)]).astype(np.int64)
    return lists[np.arange(k) % 512 // 64]


def pack_weight(w):
    k, n = w.shape
    w = f64(np.asarray(w, np.float32).astype(ml_dtypes.bfloat16)).reshape(k // 32, 32, n)
    amax = np.abs(w).max(1)
    byte = np.clip(np.where(amax > 0, np.frexp(amax)[1] - 1 + 127 - 7, 1), 1, 254)
    scaled = (w * np.exp2(127.0 - byte)[:, None, :]).reshape(k, n).astype(np.float32)
    words = np.ascontiguousarray(scaled.reshape(k // 512, 128, 4, n).transpose(0, 1, 3, 2)).astype(ml_dtypes.float8_e4m3fn).view(np.uint8)
    return words, np.ascontiguousarray(byte.astype(np.uint8).reshape(k // 512, 16, n))


def unpack_weight(words, scales):
    g, p, n, _ = words.shape
    vals = np.ascontiguousarray(words).view(ml_dtypes.float8_e4m3fn).astype(np.float64) * np.repeat(np.exp2(scales.astype(np.float64) - 127.0), 8, axis=1)[..., None]
    return vals.transpose(0, 1, 3, 2).reshape(g * 512, n)

def planes(y):
    n, m = y.shape
    v = y.astype(np.float32).astype(ml_dtypes.bfloat16).astype(np.float64).reshape(n // 32, 32, m)
    top = np.abs(v).max(1)
    byte = np.clip(np.where(top > 0, np.frexp(top)[1] - 1 + 127 - 7, 1), 1, 254)
    codes = (v * np.exp2(127.0 - byte)[:, None, :]).reshape(n, m).astype(np.float32).astype(ml_dtypes.float8_e4m3fn).view(np.uint8)
    words = codes.reshape(n // 512, 128, 4, m).transpose(0, 1, 3, 2)
    return np.ascontiguousarray(words), np.ascontiguousarray(byte.astype(np.uint8).reshape(n // 512, 16, m))


K, T, S, H = 512, 2048, 512, 512


def setup_inputs():
    n = np.random.standard_normal
    s = mx_kscale(K)[:, None]
    u = mx_kscale(S)
    packed_xT = pack_weight(n((K, T)) * s)
    packed_w1 = pack_weight(n((K, H)) / np.sqrt(K) / s)
    return {
        "x_words": packed_xT[0],
        "x_scales": packed_xT[1],
        "w1_words": packed_w1[0],
        "w1_scales": packed_w1[1],
        "ga": (np.random.uniform(0.5, 1.5, (H, 1)) * u[:, None]).astype(np.float32),
        "gb": (np.random.uniform(0.5, 1.5, (H, 1)) / u[:, None]).astype(np.float32),
        "offs": striped(np.random.permutation(T)[:S]),
        "n1": striped8(np.stack([np.random.permutation(S) for _ in range(8)])),
        "n2": striped8(np.stack([np.random.permutation(S) for _ in range(8)])),
        "n3": striped8(np.stack([np.random.permutation(S) for _ in range(8)])),
        "n4": striped8(np.stack([np.random.permutation(S) for _ in range(8)])),
        "n5": striped8(np.stack([np.random.permutation(S) for _ in range(8)])),
        "n6": striped8(np.stack([np.random.permutation(S) for _ in range(8)])),
    }


def reference(x_words, x_scales, w1_words, w1_scales, ga, gb, offs, n1, n2, n3, n4, n5, n6):
    xq = unpack_weight(x_words, x_scales)[:, unstriped(offs)]
    y = unpack_weight(w1_words, w1_scales).T @ xq
    pa = y[np.arange(H)[:, None], runs(n1, H)]
    kr = np.exp(-0.5 * ((y - pa) ** 2))
    pb = y[np.arange(H)[:, None], runs(n2, H)]
    kr2 = np.exp(-0.5 * ((y - pb) ** 2))
    z = f64(ga) * ((kr * pa + kr2 * pb) / (kr + kr2 + 0.5))
    z2 = f64(gb) * ((y - (y[np.arange(H)[:, None], runs(n3, H)])) / (np.abs(y[np.arange(H)[:, None], runs(n4, H)] - y) + 0.5))
    s = 0.0625 * ((mxq(z, 0, "e4m3").T @ mxq(z2, 0, "e4m3")))
    out_0 = s - (np.minimum(s[np.arange(S)[:, None], runs(n5, S)], s[np.arange(S)[:, None], runs(n6, S)]))
    return (out_0,) + planes(out_0)

@@ -1,0 +1,246 @@
+from contextlib import ExitStack
+
+import concourse.mybir as mybir
+from concourse.masks import make_identity
+
+F32 = mybir.dt.float32
+BF16 = mybir.dt.bfloat16
+I32 = mybir.dt.int32
+U32 = mybir.dt.uint32
+U16 = mybir.dt.uint16
+U8 = mybir.dt.uint8
+FP8X4 = mybir.dt.float8_e4m3fn_x4
+ALU = mybir.AluOpType
+ACT = mybir.ActivationFunctionType
+
+P = 128
+PACK = 4
+K, T, S, H = 512, 2048, 512, 512
+FLOPS = 2 * K * H * S + 2 * H * S * S
+TINY = 2.0 ** -100
+Z2_CHUNKS = ((0, 256), (256, 384), (384, 512))
+OUT_CHUNKS = ((0, 256), (256, 384), (384, 512))
+
+
+def tile_picked_selfkernfracunder_none_po_kernel(
+    tc, x_words, x_scales, w1_words, w1_scales, ga, gb, offs, n1, n2, n3, n4, n5, n6, out_0, out_1, out_2
+):
+    nc = tc.nc
+    with ExitStack() as ctx:
+        lists = ctx.enter_context(tc.tile_pool(name="lists", bufs=1))
+        keep = ctx.enter_context(tc.tile_pool(name="keep", bufs=1))
+        psum = ctx.enter_context(tc.psum_pool(name="psum", bufs=1))
+
+        def load_list(src, name):
+            dst = lists.tile([P, S // 16], U16, name=name)
+            nc.sync.dma_start(dst[:], src)
+            return dst
+
+        def load_scale_rows(dst, src, queues):
+            for q in range(4):
+                queues[q].dma_start(
+                    out=dst[32 * q : 32 * q + 4, :].bitcast(I32), in_=src[0, 4 * q : 4 * q + 4, :].bitcast(I32)
+                )
+
+        xs = keep.tile([P, T], U8, name="xs", align_bytes=64)
+        ws = keep.tile([P, H], U8, name="ws", align_bytes=64)
+        xs_rows = keep.tile([P, T], U8, name="xs_rows", align_bytes=64)
+        nc.vector.memset(ws[:].bitcast(I32), 0)
+        load_scale_rows(xs_rows, x_scales, [nc.scalar] * 4)
+        l_offs = load_list(offs, "l_offs")
+        xw = keep.tile([P, T], I32, name="xw", align_bytes=64)
+        nc.sync.dma_start(out=xw[:], in_=x_words[0].rearrange("p n t -> p (n t)").bitcast(I32))
+        ww = keep.tile([P, H], I32, name="ww", align_bytes=64)
+        nc.sync.dma_start(out=ww[:], in_=w1_words[0].rearrange("p n t -> p (n t)").bitcast(I32))
+        load_scale_rows(ws, w1_scales, [nc.sync, nc.scalar, nc.gpsimd, nc.gpsimd])
+        nc.vector.memset(xs[:].bitcast(I32), 0)
+        for q in range(4):
+            live = slice(32 * q, 32 * q + 4)
+            nc.vector.tensor_copy(xs[live, :].bitcast(I32), xs_rows[live, :].bitcast(I32))
+        ga_t = keep.tile([P, PACK], F32, name="ga_t")
+        gb_t = keep.tile([P, PACK], F32, name="gb_t")
+        l1, l2 = load_list(n1, "l1"), load_list(n2, "l2")
+        nc.gpsimd.dma_start(out=ga_t[:], in_=ga.rearrange("(p t) o -> p (t o)", t=PACK))
+        nc.gpsimd.dma_start(out=gb_t[:], in_=gb.rearrange("(p t) o -> p (t o)", t=PACK))
+        l4, l3, l5, l6 = [load_list(src, name) for src, name in ((n4, "l4"), (n3, "l3"), (n5, "l5"), (n6, "l6"))]
+
+        ident = keep.tile([P, P], F32, name="ident")
+        make_identity(nc, ident[:])
+        half = keep.tile([P, 1], F32, name="half")
+        nc.gpsimd.memset(half[:], 0.5)
+        y = [keep.tile([P, 2 * S], F32, name=f"y{t}") for t in range(PACK)]
+        for t in range(PACK):
+            nc.vector.memset(y[t][:, S:], 0.0)
+
+        xsg = keep.tile([P, S], U8, name="xsg", align_bytes=64)
+        nc.vector.tensor_copy(xsg[:], xs[:].indirect(l_offs[:]))
+        xg = [keep.tile([P, S // 2], U32, name=f"xg{h}", align_bytes=64) for h in range(2)]
+        for h in range(2):
+            nc.vector.tensor_copy(xg[h][:], xw[:].bitcast(U32).indirect(l_offs[:, 16 * h : 16 * (h + 1)]))
+
+        wd = keep.tile([P, H], I32, name="wd", align_bytes=64)
+        wsd = keep.tile([P, H], U8, name="wsd", align_bytes=64)
+        nc.vector.tensor_copy(
+            out=wsd[:].rearrange("p (t m) -> p m t", t=PACK), in_=ws[:].rearrange("p (m t) -> p m t", t=PACK)
+        )
+        nc.vector.tensor_copy(
+            out=wd[:].rearrange("p (t m) -> p m t", t=PACK), in_=ww[:].rearrange("p (m t) -> p m t", t=PACK)
+        )
+
+        y_ps = [psum.tile([P, S], F32, name=f"y_ps{t}", tag=f"acc{t}") for t in range(PACK)]
+        for h in range(2):
+            for t in range(PACK):
+                nc.tensor.matmul_mx(
+                    out=y_ps[t][:, 256 * h : 256 * (h + 1)],
+                    lhsT=wd[:, P * t : P * (t + 1)].bitcast(FP8X4),
+                    lhsT_scale=wsd[:, P * t : P * (t + 1)],
+                    rhs=xg[h][:].bitcast(FP8X4),
+                    rhs_scale=xsg[:, 256 * h : 256 * (h + 1)],
+                    start=True,
+                    stop=True,
+                )
+        neg_y = [keep.tile([P, S], F32, name=f"neg_y{t}") for t in range(PACK)]
+        for t in range(PACK):
+            nc.scalar.activation(y[t][:, :S], y_ps[t][:], ACT.Copy)
+            nc.scalar.activation(neg_y[t][:], y_ps[t][:], ACT.Copy, scale=-1.0)
+
+        gb_safe = keep.tile([P, PACK], F32, name="gb_safe")
+        nc.vector.tensor_scalar(gb_safe[:], gb_t[:], 0.0, TINY, ALU.is_equal, ALU.mult)
+        nc.vector.tensor_tensor(gb_safe[:], gb_safe[:], gb_t[:], ALU.add)
+        inv_gb = keep.tile([P, PACK], F32, name="inv_gb")
+        nc.vector.reciprocal(inv_gb[:], gb_safe[:])
+        half_inv_gb = keep.tile([P, PACK], F32, name="half_inv_gb")
+        nc.vector.tensor_scalar(half_inv_gb[:], inv_gb[:], 0.5, None, ALU.mult)
+        ga_signed = keep.tile([P, PACK], F32, name="ga_signed")
+        nc.vector.tensor_scalar(ga_signed[:], gb_t[:], 0.0, 2.0, ALU.is_lt, ALU.mult)
+        nc.vector.scalar_tensor_tensor(ga_signed[:], ga_signed[:], -1.0, ga_t[:], ALU.add, ALU.mult)
+
+        def turned_sum(bank, parts):
+            for b in range(PACK):
+                cols = slice(P * b, P * (b + 1))
+                for i, part in enumerate(parts):
+                    nc.tensor.matmul(
+                        bank[:, cols], lhsT=part[:, cols], rhs=ident[:], is_transpose=True,
+                        start=(i == 0), stop=(i == len(parts) - 1),
+                    )
+
+        sq = keep.tile([P, PACK, 2 * S], F32, name="sq", tag="sq_then_rsqrt")
+        num = keep.tile([P, PACK, S], F32, name="num")
+        den_ps = []
+        k_tags = (("spare0", "spare1"), ("acc0", "acc1"), ("acc2", "acc3"), ("spare0", "spare1"))
+        den_tags = ("d0", "d1", "acc0", "acc1")
+        k_all = []
+        pa = keep.tile([P, PACK, S], F32, name="pa")
+        pb = keep.tile([P, PACK, S], F32, name="pb")
+        for t in range(PACK):
+            picked = [pa[:, t, :], pb[:, t, :]]
+            k_turned = keep.tile([P, 2 * S], F32, name=f"k_turned{t}")
+            for i, lst in enumerate((l1, l2)):
+                nc.vector.tensor_copy(picked[i], y[t][:].indirect(lst[:]))
+                d_ps = psum.tile([P, S], F32, name="d_ps", tag=f"d{i}")
+                turned_sum(d_ps, (picked[i], neg_y[t]))
+                nc.scalar.activation(sq[:, t, S * i : S * (i + 1)], d_ps[:], ACT.Square)
+            nc.scalar.activation(k_turned[:], sq[:, t, :], ACT.Exp, scale=-0.5)
+            terms = [keep.tile([P, S], F32, name=f"term{t}_{i}") for i in range(2)]
+            for i in range(2):
+                k_ps = psum.tile([P, S], F32, name="k_ps", tag=k_tags[t][i])
+                turned_sum(k_ps, (k_turned[:, S * i : S * (i + 1)],))
+                nc.vector.scalar_tensor_tensor(
+                    terms[i][:], k_ps[:], ga_signed[:, t : t + 1], picked[i], ALU.mult, ALU.mult
+                )
+            k_all.append(k_turned)
+            nc.vector.tensor_tensor(num[:, t, :], terms[0][:], terms[1][:], ALU.add)
+        for t in range(PACK):
+            den = psum.tile([P, S], F32, name=f"den{t}", tag=den_tags[t])
+            turned_sum(den, (k_all[t][:, :S], k_all[t][:, S:]))
+            den_ps.append(den)
+
+        d4 = keep.tile([P, PACK, S], F32, name="d4")
+        d3 = pa
+        for t in range(PACK):
+            nc.vector.tensor_tensor(d4[:, t, :], y[t][:].indirect(l4[:]), neg_y[t][:], ALU.add)
+        for t in range(PACK):
+            nc.vector.tensor_tensor(d3[:, t, :], y[t][:].indirect(l3[:]), neg_y[t][:], ALU.add)
+
+        after_exp = keep.tile([P, 3, PACK, S], F32, name="after_exp", tag="sq_then_rsqrt")
+        rs1, rs2, abs4 = after_exp[:, 0], after_exp[:, 1], after_exp[:, 2]
+        nc.scalar.activation(abs4, d4[:], ACT.Abs)
+        for t in range(PACK):
+            nc.scalar.activation(rs1[:, t, :], den_ps[t][:], ACT.Abs_reciprocal_sqrt, bias=half[:])
+        zq = keep.tile([P, PACK * S], BF16, name="zq", align_bytes=64)
+        for c in range(2):
+            cols = slice(256 * c, 256 * (c + 1))
+            r1 = keep.tile([P, PACK, 256], F32, name=f"r1_{c}")
+            nc.scalar.activation(r1[:], rs1[:, :, cols], ACT.Square)
+            nc.vector.tensor_tensor(
+                zq[:].rearrange("p (u m t) -> p m t u", u=PACK, t=PACK)[:, 64 * c : 64 * (c + 1)],
+                num[:, :, cols].rearrange("p t (m u) -> p m t u", u=PACK),
+                r1[:].rearrange("p t (m u) -> p m t u", u=PACK),
+                ALU.mult,
+            )
+        z_codes = keep.tile([P, S], U32, name="z_codes", align_bytes=64)
+        z_scales = keep.tile([P, S], U8, name="z_scales", align_bytes=64)
+        nc.vector.quantize_mx(out=z_codes[:].bitcast(FP8X4), scales=z_scales[:], in_=zq[:])
+
+        for t in range(PACK):
+            nc.scalar.activation(
+                rs2[:, t, :], abs4[:, t, :], ACT.Abs_reciprocal_sqrt,
+                bias=half_inv_gb[:, t : t + 1], scale=inv_gb[:, t : t + 1],
+            )
+        s_ps = [psum.tile([P, S], F32, name=f"s_ps{t}", tag=tag) for t, tag in enumerate(("acc2", "acc3", "spare0", "spare1"))]
+        neg_s = [keep.tile([P, S], F32, name=f"neg_s{t}") for t in range(PACK)]
+        s_sb = [keep.tile([P, S], F32, name=f"s_sb{t}") for t in range(PACK)]
+        for c, (c0, c1) in enumerate(Z2_CHUNKS):
+            w = c1 - c0
+            r2 = keep.tile([P, PACK, w], F32, name=f"r2_{c}")
+            nc.scalar.activation(r2[:], rs2[:, :, c0:c1], ACT.Square)
+            z2q = keep.tile([P, PACK * w], BF16, name=f"z2q{c}", align_bytes=64)
+            nc.vector.tensor_tensor(
+                z2q[:].rearrange("p (a i t) -> p a t i", i=4, t=PACK),
+                d3[:, :, c0:c1].rearrange("p t (a i) -> p a t i", i=4),
+                r2[:].rearrange("p t (a i) -> p a t i", i=4),
+                ALU.mult,
+            )
+            z2_codes = keep.tile([P, w], U32, name=f"z2_codes{c}", align_bytes=64)
+            z2_scales = keep.tile([P, w], U8, name=f"z2_scales{c}", align_bytes=64)
+            nc.vector.quantize_mx(out=z2_codes[:].bitcast(FP8X4), scales=z2_scales[:], in_=z2q[:])
+            for t in range(PACK):
+                nc.tensor.matmul_mx(
+                    out=s_ps[t][:, c0:c1],
+                    lhsT=z_codes[:, P * t : P * (t + 1)].bitcast(FP8X4),
+                    lhsT_scale=z_scales[:, P * t : P * (t + 1)],
+                    rhs=z2_codes[:].bitcast(FP8X4),
+                    rhs_scale=z2_scales[:],
+                    start=True,
+                    stop=True,
+                )
+                nc.scalar.activation(neg_s[t][:, c0:c1], s_ps[t][:, c0:c1], ACT.Copy, scale=-0.0625)
+                nc.scalar.activation(s_sb[t][:, c0:c1], s_ps[t][:, c0:c1], ACT.Copy, scale=0.0625)
+
+        out_rows = out_0.rearrange("(p t) c -> p t c", t=PACK)
+        out_words = out_1[0].rearrange("p c r -> p (c r)").bitcast(I32)
+        o_scales = keep.tile([P, S], U8, name="o_scales", align_bytes=64)
+        for c, (c0, c1) in enumerate(OUT_CHUNKS):
+            w = c1 - c0
+            f = [keep.tile([P, PACK, w], F32, name=f"f{c}_{i}") for i in range(2)]
+            for t in range(PACK):
+                for i, lst in enumerate((l5, l6)):
+                    nc.vector.tensor_tensor(
+                        f[i][:, t, :], neg_s[t][:].indirect(lst[:, c0 // 16 : c1 // 16]), s_sb[t][:, c0:c1], ALU.add
+                    )
+            o = keep.tile([P, PACK, w], F32, name=f"o{c}")
+            nc.vector.tensor_tensor(o[:], f[0][:], f[1][:], ALU.max)
+            nc.sync.dma_start(out=out_rows[:, :, c0:c1], in_=o[:])
+            oq = keep.tile([P, PACK * w], BF16, name=f"oq{c}", align_bytes=64)
+            nc.scalar.copy(
+                out=oq[:].rearrange("p (a i t) -> p a t i", i=4, t=PACK),
+                in_=o[:].rearrange("p t (a i) -> p a t i", i=4),
+            )
+            o_codes = keep.tile([P, w], I32, name=f"o_codes{c}", align_bytes=64)
+            nc.vector.quantize_mx(out=o_codes[:].bitcast(FP8X4), scales=o_scales[:, c0:c1], in_=oq[:])
+            nc.sync.dma_start(out=out_words[:, c0:c1], in_=o_codes[:])
+        for q in range(4):
+            queue = nc.scalar if q % 2 else nc.sync
+            queue.dma_start(
+                out=out_2[0, 4 * q : 4 * q + 4, :].bitcast(I32), in_=o_scales[32 * q : 32 * q + 4, :].bitcast(I32)
+            )

@@ -52,7 +52,7 @@ def tile_picked_selfkernfracunder_none_po_kernel(
         nc.sync.dma_start(out=xw[:], in_=x_words[0].rearrange("p n t -> p (n t)").bitcast(I32))
         ww = keep.tile([P, H], I32, name="ww", align_bytes=64)
         nc.sync.dma_start(out=ww[:], in_=w1_words[0].rearrange("p n t -> p (n t)").bitcast(I32))
-        load_scale_rows(ws, w1_scales, [nc.sync, nc.scalar, nc.gpsimd, nc.gpsimd])
+        load_scale_rows(ws, w1_scales, [nc.sync, nc.scalar, nc.sync, nc.scalar])
         nc.vector.memset(xs[:].bitcast(I32), 0)
         for q in range(4):
             live = slice(32 * q, 32 * q + 4)
@@ -60,8 +60,8 @@ def tile_picked_selfkernfracunder_none_po_kernel(
         ga_t = keep.tile([P, PACK], F32, name="ga_t")
         gb_t = keep.tile([P, PACK], F32, name="gb_t")
         l1, l2 = load_list(n1, "l1"), load_list(n2, "l2")
-        nc.gpsimd.dma_start(out=ga_t[:], in_=ga.rearrange("(p t) o -> p (t o)", t=PACK))
-        nc.gpsimd.dma_start(out=gb_t[:], in_=gb.rearrange("(p t) o -> p (t o)", t=PACK))
+        nc.sync.dma_start(out=ga_t[:], in_=ga.rearrange("(p t) o -> p (t o)", t=PACK))
+        nc.sync.dma_start(out=gb_t[:], in_=gb.rearrange("(p t) o -> p (t o)", t=PACK))
         l4, l3, l5, l6 = [load_list(src, name) for src, name in ((n4, "l4"), (n3, "l3"), (n5, "l5"), (n6, "l6"))]
 
         ident = keep.tile([P, P], F32, name="ident")
@@ -105,15 +105,16 @@ def tile_picked_selfkernfracunder_none_po_kernel(
             nc.scalar.activation(neg_y[t][:], y_ps[t][:], ACT.Copy, scale=-1.0)
 
         gb_safe = keep.tile([P, PACK], F32, name="gb_safe")
-        nc.vector.tensor_scalar(gb_safe[:], gb_t[:], 0.0, TINY, ALU.is_equal, ALU.mult)
-        nc.vector.tensor_tensor(gb_safe[:], gb_safe[:], gb_t[:], ALU.add)
+        nc.gpsimd.tensor_scalar(gb_safe[:], gb_t[:], 0.0, TINY, ALU.is_equal, ALU.mult)
+        nc.gpsimd.tensor_tensor(gb_safe[:], gb_safe[:], gb_t[:], ALU.add)
         inv_gb = keep.tile([P, PACK], F32, name="inv_gb")
         nc.vector.reciprocal(inv_gb[:], gb_safe[:])
         half_inv_gb = keep.tile([P, PACK], F32, name="half_inv_gb")
-        nc.vector.tensor_scalar(half_inv_gb[:], inv_gb[:], 0.5, None, ALU.mult)
+        nc.gpsimd.tensor_scalar(half_inv_gb[:], inv_gb[:], 0.5, 0.0, ALU.mult, ALU.add)
         ga_signed = keep.tile([P, PACK], F32, name="ga_signed")
-        nc.vector.tensor_scalar(ga_signed[:], gb_t[:], 0.0, 2.0, ALU.is_lt, ALU.mult)
-        nc.vector.scalar_tensor_tensor(ga_signed[:], ga_signed[:], -1.0, ga_t[:], ALU.add, ALU.mult)
+        nc.gpsimd.tensor_scalar(ga_signed[:], gb_t[:], 0.0, 0.5, ALU.is_lt, ALU.subtract)
+        nc.gpsimd.tensor_scalar(ga_signed[:], ga_signed[:], 2.0, 0.0, ALU.mult, ALU.add)
+        nc.gpsimd.tensor_tensor(ga_signed[:], ga_signed[:], ga_t[:], ALU.mult)
 
         def turned_sum(bank, parts):
             for b in range(PACK):
@@ -126,33 +127,38 @@ def tile_picked_selfkernfracunder_none_po_kernel(
 
         sq = keep.tile([P, PACK, 2 * S], F32, name="sq", tag="sq_then_rsqrt")
         num = keep.tile([P, PACK, S], F32, name="num")
-        den_ps = []
-        k_tags = (("spare0", "spare1"), ("acc0", "acc1"), ("acc2", "acc3"), ("spare0", "spare1"))
-        den_tags = ("d0", "d1", "acc0", "acc1")
-        k_all = []
         pa = keep.tile([P, PACK, S], F32, name="pa")
         pb = keep.tile([P, PACK, S], F32, name="pb")
-        for t in range(PACK):
-            picked = [pa[:, t, :], pb[:, t, :]]
-            k_turned = keep.tile([P, 2 * S], F32, name=f"k_turned{t}")
-            for i, lst in enumerate((l1, l2)):
-                nc.vector.tensor_copy(picked[i], y[t][:].indirect(lst[:]))
-                d_ps = psum.tile([P, S], F32, name="d_ps", tag=f"d{i}")
-                turned_sum(d_ps, (picked[i], neg_y[t]))
+        k_turned = [keep.tile([P, 2 * S], F32, name=f"k_turned{t}") for t in range(PACK)]
+        d_tags = (("d0", "d1"), ("d2", "d3"))
+
+        def kernel_weights(t):
+            for i, (lst, picked) in enumerate(((l1, pa), (l2, pb))):
+                nc.vector.tensor_copy(picked[:, t, :], y[t][:].indirect(lst[:]))
+                d_ps = psum.tile([P, S], F32, name="d_ps", tag=d_tags[t % 2][i])
+                turned_sum(d_ps, (picked[:, t, :], neg_y[t]))
                 nc.scalar.activation(sq[:, t, S * i : S * (i + 1)], d_ps[:], ACT.Square)
-            nc.scalar.activation(k_turned[:], sq[:, t, :], ACT.Exp, scale=-0.5)
+            nc.scalar.activation(k_turned[t][:], sq[:, t, :], ACT.Exp, scale=-0.5)
+
+        def numerator(t):
             terms = [keep.tile([P, S], F32, name=f"term{t}_{i}") for i in range(2)]
-            for i in range(2):
-                k_ps = psum.tile([P, S], F32, name="k_ps", tag=k_tags[t][i])
-                turned_sum(k_ps, (k_turned[:, S * i : S * (i + 1)],))
+            for i, picked in enumerate((pa, pb)):
+                k_ps = psum.tile([P, S], F32, name="k_ps", tag=f"acc{2 * (t % 2) + i}")
+                turned_sum(k_ps, (k_turned[t][:, S * i : S * (i + 1)],))
                 nc.vector.scalar_tensor_tensor(
-                    terms[i][:], k_ps[:], ga_signed[:, t : t + 1], picked[i], ALU.mult, ALU.mult
+                    terms[i][:], k_ps[:], ga_signed[:, t : t + 1], picked[:, t, :], ALU.mult, ALU.mult
                 )
-            k_all.append(k_turned)
-            nc.vector.tensor_tensor(num[:, t, :], terms[0][:], terms[1][:], ALU.add)
+            nc.gpsimd.tensor_tensor(num[:, t, :], terms[0][:], terms[1][:], ALU.add)
+
+        for t in range(PACK + 1):
+            if t < PACK:
+                kernel_weights(t)
+            if t > 0:
+                numerator(t - 1)
+        den_ps = []
         for t in range(PACK):
-            den = psum.tile([P, S], F32, name=f"den{t}", tag=den_tags[t])
-            turned_sum(den, (k_all[t][:, :S], k_all[t][:, S:]))
+            den = psum.tile([P, S], F32, name=f"den{t}", tag=f"d{t}")
+            turned_sum(den, (k_turned[t][:, :S], k_turned[t][:, S:]))
             den_ps.append(den)
 
         d4 = keep.tile([P, PACK, S], F32, name="d4")
@@ -187,7 +193,7 @@ def tile_picked_selfkernfracunder_none_po_kernel(
                 rs2[:, t, :], abs4[:, t, :], ACT.Abs_reciprocal_sqrt,
                 bias=half_inv_gb[:, t : t + 1], scale=inv_gb[:, t : t + 1],
             )
-        s_ps = [psum.tile([P, S], F32, name=f"s_ps{t}", tag=tag) for t, tag in enumerate(("acc2", "acc3", "spare0", "spare1"))]
+        s_ps = [psum.tile([P, S], F32, name=f"s_ps{t}", tag=f"acc{t}") for t in range(PACK)]
         neg_s = [keep.tile([P, S], F32, name=f"neg_s{t}") for t in range(PACK)]
         s_sb = [keep.tile([P, S], F32, name=f"s_sb{t}") for t in range(PACK)]
         for c, (c0, c1) in enumerate(Z2_CHUNKS):

@@ -53,10 +53,14 @@ def tile_picked_selfkernfracunder_none_po_kernel(
         ww = keep.tile([P, H], I32, name="ww", align_bytes=64)
         nc.sync.dma_start(out=ww[:], in_=w1_words[0].rearrange("p n t -> p (n t)").bitcast(I32))
         load_scale_rows(ws, w1_scales, [nc.sync, nc.scalar, nc.sync, nc.scalar])
-        nc.vector.memset(xs[:].bitcast(I32), 0)
-        for q in range(4):
-            live = slice(32 * q, 32 * q + 4)
-            nc.vector.tensor_copy(xs[live, :].bitcast(I32), xs_rows[live, :].bitcast(I32))
+
+        def fill_plane(plane, rows):
+            nc.vector.memset(plane[:].bitcast(I32), 0)
+            for q in range(4):
+                live = slice(32 * q, 32 * q + 4)
+                nc.vector.tensor_copy(plane[live, :].bitcast(I32), rows[live, :].bitcast(I32))
+
+        fill_plane(xs, xs_rows)
         ga_t = keep.tile([P, PACK], F32, name="ga_t")
         gb_t = keep.tile([P, PACK], F32, name="gb_t")
         l1, l2 = load_list(n1, "l1"), load_list(n2, "l2")
@@ -74,9 +78,8 @@ def tile_picked_selfkernfracunder_none_po_kernel(
 
         xsg = keep.tile([P, S], U8, name="xsg", align_bytes=64)
         nc.vector.tensor_copy(xsg[:], xs[:].indirect(l_offs[:]))
-        xg = [keep.tile([P, S // 2], U32, name=f"xg{h}", align_bytes=64) for h in range(2)]
-        for h in range(2):
-            nc.vector.tensor_copy(xg[h][:], xw[:].bitcast(U32).indirect(l_offs[:, 16 * h : 16 * (h + 1)]))
+        xg = keep.tile([P, S], U32, name="xg", align_bytes=64)
+        nc.vector.tensor_copy(xg[:], xw[:].bitcast(U32).indirect(l_offs[:]))
 
         wd = keep.tile([P, H], I32, name="wd", align_bytes=64)
         wsd = keep.tile([P, H], U8, name="wsd", align_bytes=64)
@@ -88,20 +91,20 @@ def tile_picked_selfkernfracunder_none_po_kernel(
         )
 
         y_ps = [psum.tile([P, S], F32, name=f"y_ps{t}", tag=f"acc{t}") for t in range(PACK)]
-        for h in range(2):
-            for t in range(PACK):
-                nc.tensor.matmul_mx(
-                    out=y_ps[t][:, 256 * h : 256 * (h + 1)],
-                    lhsT=wd[:, P * t : P * (t + 1)].bitcast(FP8X4),
-                    lhsT_scale=wsd[:, P * t : P * (t + 1)],
-                    rhs=xg[h][:].bitcast(FP8X4),
-                    rhs_scale=xsg[:, 256 * h : 256 * (h + 1)],
-                    start=True,
-                    stop=True,
-                )
+        for t in range(PACK):
+            nc.tensor.matmul_mx(
+                out=y_ps[t][:],
+                lhsT=wd[:, P * t : P * (t + 1)].bitcast(FP8X4),
+                lhsT_scale=wsd[:, P * t : P * (t + 1)],
+                rhs=xg[:].bitcast(FP8X4),
+                rhs_scale=xsg[:],
+                start=True,
+                stop=True,
+            )
         neg_y = [keep.tile([P, S], F32, name=f"neg_y{t}") for t in range(PACK)]
         for t in range(PACK):
             nc.scalar.activation(y[t][:, :S], y_ps[t][:], ACT.Copy)
+        for t in range(PACK):
             nc.scalar.activation(neg_y[t][:], y_ps[t][:], ACT.Copy, scale=-1.0)
 
         gb_safe = keep.tile([P, PACK], F32, name="gb_safe")
@@ -127,15 +130,15 @@ def tile_picked_selfkernfracunder_none_po_kernel(
 
         sq = keep.tile([P, PACK, 2 * S], F32, name="sq", tag="sq_then_rsqrt")
         num = keep.tile([P, PACK, S], F32, name="num")
-        pa = keep.tile([P, PACK, S], F32, name="pa")
+        pa = keep.tile([P, PACK, S], F32, name="pa", tag="pa")
         pb = keep.tile([P, PACK, S], F32, name="pb")
         k_turned = [keep.tile([P, 2 * S], F32, name=f"k_turned{t}") for t in range(PACK)]
-        d_tags = (("d0", "d1"), ("d2", "d3"))
+        den_ps = []
 
         def kernel_weights(t):
             for i, (lst, picked) in enumerate(((l1, pa), (l2, pb))):
                 nc.vector.tensor_copy(picked[:, t, :], y[t][:].indirect(lst[:]))
-                d_ps = psum.tile([P, S], F32, name="d_ps", tag=d_tags[t % 2][i])
+                d_ps = psum.tile([P, S], F32, name="d_ps", tag=f"d{i}")
                 turned_sum(d_ps, (picked[:, t, :], neg_y[t]))
                 nc.scalar.activation(sq[:, t, S * i : S * (i + 1)], d_ps[:], ACT.Square)
             nc.scalar.activation(k_turned[t][:], sq[:, t, :], ACT.Exp, scale=-0.5)
@@ -143,26 +146,32 @@ def tile_picked_selfkernfracunder_none_po_kernel(
         def numerator(t):
             terms = [keep.tile([P, S], F32, name=f"term{t}_{i}") for i in range(2)]
             for i, picked in enumerate((pa, pb)):
-                k_ps = psum.tile([P, S], F32, name="k_ps", tag=f"acc{2 * (t % 2) + i}")
+                k_ps = psum.tile([P, S], F32, name="k_ps", tag=(("k0", "k1"), ("acc2", "acc3"))[t % 2][i])
                 turned_sum(k_ps, (k_turned[t][:, S * i : S * (i + 1)],))
                 nc.vector.scalar_tensor_tensor(
                     terms[i][:], k_ps[:], ga_signed[:, t : t + 1], picked[:, t, :], ALU.mult, ALU.mult
                 )
-            nc.gpsimd.tensor_tensor(num[:, t, :], terms[0][:], terms[1][:], ALU.add)
+            adder = nc.gpsimd if t < PACK - 1 else nc.vector
+            adder.tensor_tensor(num[:, t, :], terms[0][:], terms[1][:], ALU.add)
 
-        for t in range(PACK + 1):
-            if t < PACK:
-                kernel_weights(t)
-            if t > 0:
-                numerator(t - 1)
-        den_ps = []
-        for t in range(PACK):
-            den = psum.tile([P, S], F32, name=f"den{t}", tag=f"d{t}")
+        def denominator(t):
+            den = psum.tile([P, S], F32, name=f"den{t}", tag=("acc0", "acc1", "d0", "d1")[t])
             turned_sum(den, (k_turned[t][:, :S], k_turned[t][:, S:]))
             den_ps.append(den)
 
+        kernel_weights(0)
+        kernel_weights(1)
+        kernel_weights(2)
+        kernel_weights(3)
+        numerator(0)
+        numerator(1)
+        for t in range(PACK):
+            denominator(t)
+        numerator(2)
+        numerator(3)
+
         d4 = keep.tile([P, PACK, S], F32, name="d4")
-        d3 = pa
+        d3 = keep.tile([P, PACK, S], F32, name="d3", tag="pa")
         for t in range(PACK):
             nc.vector.tensor_tensor(d4[:, t, :], y[t][:].indirect(l4[:]), neg_y[t][:], ALU.add)
         for t in range(PACK):
@@ -170,7 +179,6 @@ def tile_picked_selfkernfracunder_none_po_kernel(
 
         after_exp = keep.tile([P, 3, PACK, S], F32, name="after_exp", tag="sq_then_rsqrt")
         rs1, rs2, abs4 = after_exp[:, 0], after_exp[:, 1], after_exp[:, 2]
-        nc.scalar.activation(abs4, d4[:], ACT.Abs)
         for t in range(PACK):
             nc.scalar.activation(rs1[:, t, :], den_ps[t][:], ACT.Abs_reciprocal_sqrt, bias=half[:])
         zq = keep.tile([P, PACK * S], BF16, name="zq", align_bytes=64)
@@ -188,12 +196,13 @@ def tile_picked_selfkernfracunder_none_po_kernel(
         z_scales = keep.tile([P, S], U8, name="z_scales", align_bytes=64)
         nc.vector.quantize_mx(out=z_codes[:].bitcast(FP8X4), scales=z_scales[:], in_=zq[:])
 
+        nc.scalar.activation(abs4, d4[:], ACT.Abs)
         for t in range(PACK):
             nc.scalar.activation(
                 rs2[:, t, :], abs4[:, t, :], ACT.Abs_reciprocal_sqrt,
                 bias=half_inv_gb[:, t : t + 1], scale=inv_gb[:, t : t + 1],
             )
-        s_ps = [psum.tile([P, S], F32, name=f"s_ps{t}", tag=f"acc{t}") for t in range(PACK)]
+        s_ps = [psum.tile([P, S], F32, name=f"s_ps{t}", tag=("k0", "k1", "acc2", "acc3")[t]) for t in range(PACK)]
         neg_s = [keep.tile([P, S], F32, name=f"neg_s{t}") for t in range(PACK)]
         s_sb = [keep.tile([P, S], F32, name=f"s_sb{t}") for t in range(PACK)]
         for c, (c0, c1) in enumerate(Z2_CHUNKS):
@@ -220,8 +229,11 @@ def tile_picked_selfkernfracunder_none_po_kernel(
                     start=True,
                     stop=True,
                 )
-                nc.scalar.activation(neg_s[t][:, c0:c1], s_ps[t][:, c0:c1], ACT.Copy, scale=-0.0625)
-                nc.scalar.activation(s_sb[t][:, c0:c1], s_ps[t][:, c0:c1], ACT.Copy, scale=0.0625)
+            nc.scalar.activation(neg_s[0][:, c0:c1], s_ps[0][:, c0:c1], ACT.Copy, scale=-0.0625)
+            nc.scalar.activation(s_sb[0][:, c0:c1], s_ps[0][:, c0:c1], ACT.Copy, scale=0.0625)
+        for t in range(1, PACK):
+            nc.scalar.activation(neg_s[t][:], s_ps[t][:], ACT.Copy, scale=-0.0625)
+            nc.scalar.activation(s_sb[t][:], s_ps[t][:], ACT.Copy, scale=0.0625)
 
         out_rows = out_0.rearrange("(p t) c -> p t c", t=PACK)
         out_words = out_1[0].rearrange("p c r -> p (c r)").bitcast(I32)
@@ -235,16 +247,14 @@ def tile_picked_selfkernfracunder_none_po_kernel(
                         f[i][:, t, :], neg_s[t][:].indirect(lst[:, c0 // 16 : c1 // 16]), s_sb[t][:, c0:c1], ALU.add
                     )
             o = keep.tile([P, PACK, w], F32, name=f"o{c}")
+            oq = keep.tile([P, PACK * w], BF16, name=f"oq{c}", align_bytes=64)
+            oq_view = oq[:].rearrange("p (a i t) -> p a t i", i=4, t=PACK)
             nc.vector.tensor_tensor(o[:], f[0][:], f[1][:], ALU.max)
             nc.sync.dma_start(out=out_rows[:, :, c0:c1], in_=o[:])
-            oq = keep.tile([P, PACK * w], BF16, name=f"oq{c}", align_bytes=64)
-            nc.scalar.copy(
-                out=oq[:].rearrange("p (a i t) -> p a t i", i=4, t=PACK),
-                in_=o[:].rearrange("p t (a i) -> p a t i", i=4),
-            )
+            nc.scalar.copy(out=oq_view, in_=o[:].rearrange("p t (a i) -> p a t i", i=4))
             o_codes = keep.tile([P, w], I32, name=f"o_codes{c}", align_bytes=64)
             nc.vector.quantize_mx(out=o_codes[:].bitcast(FP8X4), scales=o_scales[:, c0:c1], in_=oq[:])
-            nc.sync.dma_start(out=out_words[:, c0:c1], in_=o_codes[:])
+            nc.scalar.dma_start(out=out_words[:, c0:c1], in_=o_codes[:])
         for q in range(4):
             queue = nc.scalar if q % 2 else nc.sync
             queue.dma_start(

from contextlib import ExitStack

import concourse.mybir as mybir
from concourse.masks import make_identity

F32 = mybir.dt.float32
BF16 = mybir.dt.bfloat16
I32 = mybir.dt.int32
U32 = mybir.dt.uint32
U16 = mybir.dt.uint16
U8 = mybir.dt.uint8
FP8X4 = mybir.dt.float8_e4m3fn_x4
ALU = mybir.AluOpType
ACT = mybir.ActivationFunctionType

P = 128
PACK = 4
K, T, S, H = 512, 2048, 512, 512
FLOPS = 2 * K * H * S + 2 * H * S * S
TINY = 2.0 ** -100
Z2_CHUNKS = ((0, 256), (256, 384), (384, 512))
OUT_CHUNKS = ((0, 256), (256, 384), (384, 512))


def tile_picked_selfkernfracunder_none_po_kernel(
    tc, x_words, x_scales, w1_words, w1_scales, ga, gb, offs, n1, n2, n3, n4, n5, n6, out_0, out_1, out_2
):
    nc = tc.nc
    with ExitStack() as ctx:
        lists = ctx.enter_context(tc.tile_pool(name="lists", bufs=1))
        keep = ctx.enter_context(tc.tile_pool(name="keep", bufs=1))
        psum = ctx.enter_context(tc.psum_pool(name="psum", bufs=1))

        def load_list(src, name):
            dst = lists.tile([P, S // 16], U16, name=name)
            nc.sync.dma_start(dst[:], src)
            return dst

        def load_scale_rows(dst, src, queues):
            for q in range(4):
                queues[q].dma_start(
                    out=dst[32 * q : 32 * q + 4, :].bitcast(I32), in_=src[0, 4 * q : 4 * q + 4, :].bitcast(I32)
                )

        xs = keep.tile([P, T], U8, name="xs", align_bytes=64)
        ws = keep.tile([P, H], U8, name="ws", align_bytes=64)
        xs_rows = keep.tile([P, T], U8, name="xs_rows", align_bytes=64)
        nc.vector.memset(ws[:].bitcast(I32), 0)
        load_scale_rows(xs_rows, x_scales, [nc.scalar] * 4)
        l_offs = load_list(offs, "l_offs")
        xw = keep.tile([P, T], I32, name="xw", align_bytes=64)
        nc.sync.dma_start(out=xw[:], in_=x_words[0].rearrange("p n t -> p (n t)").bitcast(I32))
        ww = keep.tile([P, H], I32, name="ww", align_bytes=64)
        nc.sync.dma_start(out=ww[:], in_=w1_words[0].rearrange("p n t -> p (n t)").bitcast(I32))
        load_scale_rows(ws, w1_scales, [nc.sync, nc.scalar, nc.sync, nc.scalar])

        def fill_plane(plane, rows):
            nc.vector.memset(plane[:].bitcast(I32), 0)
            for q in range(4):
                live = slice(32 * q, 32 * q + 4)
                nc.vector.tensor_copy(plane[live, :].bitcast(I32), rows[live, :].bitcast(I32))

        fill_plane(xs, xs_rows)
        ga_t = keep.tile([P, PACK], F32, name="ga_t")
        gb_t = keep.tile([P, PACK], F32, name="gb_t")
        l1, l2 = load_list(n1, "l1"), load_list(n2, "l2")
        nc.sync.dma_start(out=ga_t[:], in_=ga.rearrange("(p t) o -> p (t o)", t=PACK))
        nc.sync.dma_start(out=gb_t[:], in_=gb.rearrange("(p t) o -> p (t o)", t=PACK))
        l4, l3, l5, l6 = [load_list(src, name) for src, name in ((n4, "l4"), (n3, "l3"), (n5, "l5"), (n6, "l6"))]

        ident = keep.tile([P, P], F32, name="ident")
        make_identity(nc, ident[:])
        half = keep.tile([P, 1], F32, name="half")
        nc.gpsimd.memset(half[:], 0.5)
        y = [keep.tile([P, 2 * S], F32, name=f"y{t}") for t in range(PACK)]
        for t in range(PACK):
            nc.vector.memset(y[t][:, S:], 0.0)

        xsg = keep.tile([P, S], U8, name="xsg", align_bytes=64)
        nc.vector.tensor_copy(xsg[:], xs[:].indirect(l_offs[:]))
        xg = keep.tile([P, S], U32, name="xg", align_bytes=64)
        nc.vector.tensor_copy(xg[:], xw[:].bitcast(U32).indirect(l_offs[:]))

        wd = keep.tile([P, H], I32, name="wd", align_bytes=64)
        wsd = keep.tile([P, H], U8, name="wsd", align_bytes=64)
        nc.vector.tensor_copy(
            out=wsd[:].rearrange("p (t m) -> p m t", t=PACK), in_=ws[:].rearrange("p (m t) -> p m t", t=PACK)
        )
        nc.vector.tensor_copy(
            out=wd[:].rearrange("p (t m) -> p m t", t=PACK), in_=ww[:].rearrange("p (m t) -> p m t", t=PACK)
        )

        y_ps = [psum.tile([P, S], F32, name=f"y_ps{t}", tag=f"acc{t}") for t in range(PACK)]
        for t in range(PACK):
            nc.tensor.matmul_mx(
                out=y_ps[t][:],
                lhsT=wd[:, P * t : P * (t + 1)].bitcast(FP8X4),
                lhsT_scale=wsd[:, P * t : P * (t + 1)],
                rhs=xg[:].bitcast(FP8X4),
                rhs_scale=xsg[:],
                start=True,
                stop=True,
            )
        neg_y = [keep.tile([P, S], F32, name=f"neg_y{t}") for t in range(PACK)]
        for t in range(PACK):
            nc.scalar.activation(y[t][:, :S], y_ps[t][:], ACT.Copy)
        for t in range(PACK):
            nc.scalar.activation(neg_y[t][:], y_ps[t][:], ACT.Copy, scale=-1.0)

        gb_safe = keep.tile([P, PACK], F32, name="gb_safe")
        nc.gpsimd.tensor_scalar(gb_safe[:], gb_t[:], 0.0, TINY, ALU.is_equal, ALU.mult)
        nc.gpsimd.tensor_tensor(gb_safe[:], gb_safe[:], gb_t[:], ALU.add)
        inv_gb = keep.tile([P, PACK], F32, name="inv_gb")
        nc.vector.reciprocal(inv_gb[:], gb_safe[:])
        half_inv_gb = keep.tile([P, PACK], F32, name="half_inv_gb")
        nc.gpsimd.tensor_scalar(half_inv_gb[:], inv_gb[:], 0.5, 0.0, ALU.mult, ALU.add)
        ga_signed = keep.tile([P, PACK], F32, name="ga_signed")
        nc.gpsimd.tensor_scalar(ga_signed[:], gb_t[:], 0.0, 0.5, ALU.is_lt, ALU.subtract)
        nc.gpsimd.tensor_scalar(ga_signed[:], ga_signed[:], 2.0, 0.0, ALU.mult, ALU.add)
        nc.gpsimd.tensor_tensor(ga_signed[:], ga_signed[:], ga_t[:], ALU.mult)

        def turned_sum(bank, parts):
            for b in range(PACK):
                cols = slice(P * b, P * (b + 1))
                for i, part in enumerate(parts):
                    nc.tensor.matmul(
                        bank[:, cols], lhsT=part[:, cols], rhs=ident[:], is_transpose=True,
                        start=(i == 0), stop=(i == len(parts) - 1),
                    )

        sq = keep.tile([P, PACK, 2 * S], F32, name="sq", tag="sq_then_rsqrt")
        num = keep.tile([P, PACK, S], F32, name="num")
        pa = keep.tile([P, PACK, S], F32, name="pa", tag="pa")
        pb = keep.tile([P, PACK, S], F32, name="pb")
        k_turned = [keep.tile([P, 2 * S], F32, name=f"k_turned{t}") for t in range(PACK)]
        den_ps = []

        def kernel_weights(t):
            for i, (lst, picked) in enumerate(((l1, pa), (l2, pb))):
                nc.vector.tensor_copy(picked[:, t, :], y[t][:].indirect(lst[:]))
                d_ps = psum.tile([P, S], F32, name="d_ps", tag=f"d{i}")
                turned_sum(d_ps, (picked[:, t, :], neg_y[t]))
                nc.scalar.activation(sq[:, t, S * i : S * (i + 1)], d_ps[:], ACT.Square)
            nc.scalar.activation(k_turned[t][:], sq[:, t, :], ACT.Exp, scale=-0.5)

        def numerator(t):
            terms = [keep.tile([P, S], F32, name=f"term{t}_{i}") for i in range(2)]
            for i, picked in enumerate((pa, pb)):
                k_ps = psum.tile([P, S], F32, name="k_ps", tag=(("k0", "k1"), ("acc2", "acc3"))[t % 2][i])
                turned_sum(k_ps, (k_turned[t][:, S * i : S * (i + 1)],))
                nc.vector.scalar_tensor_tensor(
                    terms[i][:], k_ps[:], ga_signed[:, t : t + 1], picked[:, t, :], ALU.mult, ALU.mult
                )
            adder = nc.gpsimd if t < PACK - 1 else nc.vector
            adder.tensor_tensor(num[:, t, :], terms[0][:], terms[1][:], ALU.add)

        def denominator(t):
            den = psum.tile([P, S], F32, name=f"den{t}", tag=("acc0", "acc1", "d0", "d1")[t])
            turned_sum(den, (k_turned[t][:, :S], k_turned[t][:, S:]))
            den_ps.append(den)

        kernel_weights(0)
        kernel_weights(1)
        kernel_weights(2)
        kernel_weights(3)
        numerator(0)
        numerator(1)
        for t in range(PACK):
            denominator(t)
        numerator(2)
        numerator(3)

        d4 = keep.tile([P, PACK, S], F32, name="d4")
        d3 = keep.tile([P, PACK, S], F32, name="d3", tag="pa")
        for t in range(PACK):
            nc.vector.tensor_tensor(d4[:, t, :], y[t][:].indirect(l4[:]), neg_y[t][:], ALU.add)
        for t in range(PACK):
            nc.vector.tensor_tensor(d3[:, t, :], y[t][:].indirect(l3[:]), neg_y[t][:], ALU.add)

        after_exp = keep.tile([P, 3, PACK, S], F32, name="after_exp", tag="sq_then_rsqrt")
        rs1, rs2, abs4 = after_exp[:, 0], after_exp[:, 1], after_exp[:, 2]
        for t in range(PACK):
            nc.scalar.activation(rs1[:, t, :], den_ps[t][:], ACT.Abs_reciprocal_sqrt, bias=half[:])
        zq = keep.tile([P, PACK * S], BF16, name="zq", align_bytes=64)
        for c in range(2):
            cols = slice(256 * c, 256 * (c + 1))
            r1 = keep.tile([P, PACK, 256], F32, name=f"r1_{c}")
            nc.scalar.activation(r1[:], rs1[:, :, cols], ACT.Square)
            nc.vector.tensor_tensor(
                zq[:].rearrange("p (u m t) -> p m t u", u=PACK, t=PACK)[:, 64 * c : 64 * (c + 1)],
                num[:, :, cols].rearrange("p t (m u) -> p m t u", u=PACK),
                r1[:].rearrange("p t (m u) -> p m t u", u=PACK),
                ALU.mult,
            )
        z_codes = keep.tile([P, S], U32, name="z_codes", align_bytes=64)
        z_scales = keep.tile([P, S], U8, name="z_scales", align_bytes=64)
        nc.vector.quantize_mx(out=z_codes[:].bitcast(FP8X4), scales=z_scales[:], in_=zq[:])

        nc.scalar.activation(abs4, d4[:], ACT.Abs)
        for t in range(PACK):
            nc.scalar.activation(
                rs2[:, t, :], abs4[:, t, :], ACT.Abs_reciprocal_sqrt,
                bias=half_inv_gb[:, t : t + 1], scale=inv_gb[:, t : t + 1],
            )
        s_ps = [psum.tile([P, S], F32, name=f"s_ps{t}", tag=("k0", "k1", "acc2", "acc3")[t]) for t in range(PACK)]
        neg_s = [keep.tile([P, S], F32, name=f"neg_s{t}") for t in range(PACK)]
        s_sb = [keep.tile([P, S], F32, name=f"s_sb{t}") for t in range(PACK)]
        for c, (c0, c1) in enumerate(Z2_CHUNKS):
            w = c1 - c0
            r2 = keep.tile([P, PACK, w], F32, name=f"r2_{c}")
            nc.scalar.activation(r2[:], rs2[:, :, c0:c1], ACT.Square)
            z2q = keep.tile([P, PACK * w], BF16, name=f"z2q{c}", align_bytes=64)
            nc.vector.tensor_tensor(
                z2q[:].rearrange("p (a i t) -> p a t i", i=4, t=PACK),
                d3[:, :, c0:c1].rearrange("p t (a i) -> p a t i", i=4),
                r2[:].rearrange("p t (a i) -> p a t i", i=4),
                ALU.mult,
            )
            z2_codes = keep.tile([P, w], U32, name=f"z2_codes{c}", align_bytes=64)
            z2_scales = keep.tile([P, w], U8, name=f"z2_scales{c}", align_bytes=64)
            nc.vector.quantize_mx(out=z2_codes[:].bitcast(FP8X4), scales=z2_scales[:], in_=z2q[:])
            for t in range(PACK):
                nc.tensor.matmul_mx(
                    out=s_ps[t][:, c0:c1],
                    lhsT=z_codes[:, P * t : P * (t + 1)].bitcast(FP8X4),
                    lhsT_scale=z_scales[:, P * t : P * (t + 1)],
                    rhs=z2_codes[:].bitcast(FP8X4),
                    rhs_scale=z2_scales[:],
                    start=True,
                    stop=True,
                )
            nc.scalar.activation(neg_s[0][:, c0:c1], s_ps[0][:, c0:c1], ACT.Copy, scale=-0.0625)
            nc.scalar.activation(s_sb[0][:, c0:c1], s_ps[0][:, c0:c1], ACT.Copy, scale=0.0625)
        for t in range(1, PACK):
            nc.scalar.activation(neg_s[t][:], s_ps[t][:], ACT.Copy, scale=-0.0625)
            nc.scalar.activation(s_sb[t][:], s_ps[t][:], ACT.Copy, scale=0.0625)

        out_rows = out_0.rearrange("(p t) c -> p t c", t=PACK)
        out_words = out_1[0].rearrange("p c r -> p (c r)").bitcast(I32)
        o_scales = keep.tile([P, S], U8, name="o_scales", align_bytes=64)
        for c, (c0, c1) in enumerate(OUT_CHUNKS):
            w = c1 - c0
            f = [keep.tile([P, PACK, w], F32, name=f"f{c}_{i}") for i in range(2)]
            for t in range(PACK):
                for i, lst in enumerate((l5, l6)):
                    nc.vector.tensor_tensor(
                        f[i][:, t, :], neg_s[t][:].indirect(lst[:, c0 // 16 : c1 // 16]), s_sb[t][:, c0:c1], ALU.add
                    )
            o = keep.tile([P, PACK, w], F32, name=f"o{c}")
            oq = keep.tile([P, PACK * w], BF16, name=f"oq{c}", align_bytes=64)
            oq_view = oq[:].rearrange("p (a i t) -> p a t i", i=4, t=PACK)
            nc.vector.tensor_tensor(o[:], f[0][:], f[1][:], ALU.max)
            nc.sync.dma_start(out=out_rows[:, :, c0:c1], in_=o[:])
            nc.scalar.copy(out=oq_view, in_=o[:].rearrange("p t (a i) -> p a t i", i=4))
            o_codes = keep.tile([P, w], I32, name=f"o_codes{c}", align_bytes=64)
            nc.vector.quantize_mx(out=o_codes[:].bitcast(FP8X4), scales=o_scales[:, c0:c1], in_=oq[:])
            nc.scalar.dma_start(out=out_words[:, c0:c1], in_=o_codes[:])
        for q in range(4):
            queue = nc.scalar if q % 2 else nc.sync
            queue.dma_start(
                out=out_2[0, 4 * q : 4 * q + 4, :].bitcast(I32), in_=o_scales[32 * q : 32 * q + 4, :].bitcast(I32)
            )
